import numpy as np
import ml_dtypes


def mxq(x, axis, fmt="e4m3"):
    dtype, down = {"e4m3": (ml_dtypes.float8_e4m3fn, 7), "e5m2": (ml_dtypes.float8_e5m2, 14)}[fmt]
    v = np.moveaxis(np.asarray(x, np.float32).astype(ml_dtypes.bfloat16).astype(np.float64), axis, -1)
    blocks = v.reshape(v.shape[:-1] + (-1, 32))
    amax = np.abs(blocks).max(-1, keepdims=True)
    byte = np.maximum(np.where(amax > 0, np.frexp(amax)[1] - 1 + 127, 0) - down, 1)
    scale = np.exp2(byte - 127.0)
    codes = (blocks / scale).astype(np.float32).astype(dtype).astype(np.float64)
    return np.moveaxis((codes * scale).reshape(v.shape), -1, axis)


WIDE = False


def mx_kscale(k):
    if not WIDE:
        return np.ones(k)
    levels = np.array([10, -10, 5, -5, 0])
    if k % 512:
        return np.exp2(np.random.permutation(np.resize(levels, k // 32))).repeat(32)
    a = np.empty((k // 512, 16))
    for p in range(k // 512):
        a[p, :8] = np.random.permutation(np.resize(levels, 8))
        for g in range(8):
            far = levels[np.abs(levels - a[p, g]) >= 10]
            a[p, g + 8] = far[np.random.randint(len(far))]
    return np.exp2(a.ravel()).repeat(32)


def f64(x):
    return np.asarray(x).astype(np.float64)


def striped(idx):
    return np.tile(idx.reshape(-1, 16).T, (8, 1)).astype(np.uint16)


def unstriped(offs):
    return offs[:16].T.reshape(-1).astype(np.int64)


E2M1 = np.array([0.0, 0.5, 1.0, 1.5, 2.0, 3.0, 4.0, 6.0, -0.0, -0.5, -1.0, -1.5, -2.0, -3.0, -4.0, -6.0])


def pack_weight(w, fmt):
    k, n = w.shape
    w = f64(np.asarray(w, np.float32).astype(ml_dtypes.bfloat16)).reshape(k // 32, 32, n)
    amax = np.abs(w).max(1)
    if fmt == "e4m3":
        byte = np.frexp(amax)[1] - 1 + 127 - 7
    else:
        mant, ex = np.frexp(amax / 6.0)
        byte = np.where(mant > 0.5, ex, ex - 1) + 127
    byte = np.clip(np.where(amax > 0, byte, 1), 1, 254)
    scaled = (w * np.exp2(127.0 - byte)[:, None, :]).reshape(k, n).astype(np.float32)
    by_word = np.ascontiguousarray(scaled.reshape(k // 512, 128, 4, n).transpose(0, 1, 3, 2))
    if fmt == "e4m3":
        words = by_word.astype(ml_dtypes.float8_e4m3fn).view(np.uint8)
    else:
        c = by_word.astype(ml_dtypes.float4_e2m1fn).view(np.uint8) & 0xF
        words = (c[..., 0::2] | (c[..., 1::2] << 4)).reshape(k // 512, 128, 2 * n)
    return np.ascontiguousarray(words), np.ascontiguousarray(byte.astype(np.uint8).reshape(k // 512, 16, n))


def unpack_weight(words, scales, fmt):
    g, _, n = scales.shape
    words = np.ascontiguousarray(words).reshape(g, 128, n, -1)
    if fmt == "e4m3":
        vals = words.view(ml_dtypes.float8_e4m3fn).astype(np.float64)
    else:
        nib = np.empty((g, 128, n, 4), np.uint8)
        nib[..., 0::2] = words & 0xF
        nib[..., 1::2] = words >> 4
        vals = E2M1[nib]
    vals = vals * np.repeat(np.exp2(scales.astype(np.float64) - 127.0), 8, axis=1)[..., None]
    return vals.transpose(0, 1, 3, 2).reshape(g * 512, n)


def gelu(v):
    return 0.5 * v * (1.0 + np.tanh(np.sqrt(2.0 / np.pi) * (v + 0.044715 * v**3)))


K, T, S, H, N, P1, P2, P3 = 1024, 4096, 2048, 512, 512, 1024, 512, 256

def setup_inputs():
    n = np.random.standard_normal
    s = mx_kscale(K)[:, None]
    u = mx_kscale(H)[:, None]
    tab_words, tab_scales = pack_weight(n((K, T)) * s, "e4m3")
    w4_words, w4_scales = pack_weight(0.6 * n((H, N)) / np.sqrt(H) / u, "e2m1")
    return {
        "tab_words": tab_words, "tab_scales": tab_scales,
        "offs": striped(np.random.permutation(T)[:S]),
        "w1": (0.54 * n((K, H)) / np.sqrt(K) / s).astype(np.float32),
        "pos1": striped(np.random.permutation(S)[:P1]),
        "pos2": striped(np.random.permutation(S)[:P1]),
        "pos3": striped(np.random.permutation(P1)[:P2]),
        "pos4": striped(np.random.permutation(P1)[:P2]),
        "pos5": striped(np.random.permutation(P2)[:P3]),
        "pos6": striped(np.random.permutation(P2)[:P3]),
        "gain": (np.exp(0.3 * n(H)) * u[:, 0]).astype(np.float32),
        "w4_words": w4_words, "w4_scales": w4_scales,
        "vac": np.exp(0.4 * n((N, P3))).astype(np.float32),
    }

def reference(tab_words, tab_scales, offs, w1, pos1, pos2, pos3, pos4, pos5, pos6, gain, w4_words, w4_scales, vac):
    v = unpack_weight(tab_words, tab_scales, "e4m3")[:, unstriped(offs)]
    h = np.cos(mxq(f64(w1), 0, "e4m3").T @ v)
    a1 = h[:, unstriped(pos1)] * h[:, unstriped(pos2)]
    a2 = a1[:, unstriped(pos3)] + a1[:, unstriped(pos4)]
    a3 = np.maximum(a2[:, unstriped(pos5)], a2[:, unstriped(pos6)])
    x = mxq(a3 * f64(gain)[:, None], 0, "e4m3")
    w4 = unpack_weight(w4_words, w4_scales, "e2m1")
    y = w4.T @ x
    return np.tanh(y) * f64(vac)

@@ -1,0 +1,256 @@
+import math
+from contextlib import ExitStack
+
+import concourse.mybir as mybir
+
+K, T, S, H, N, P1, P2, P3 = 1024, 4096, 2048, 512, 512, 1024, 512, 256
+FLOPS = 2 * K * H * S + 2 * H * N * P3
+
+F32 = mybir.dt.float32
+BF16 = mybir.dt.bfloat16
+I32 = mybir.dt.int32
+U32 = mybir.dt.uint32
+U16 = mybir.dt.uint16
+U8 = mybir.dt.uint8
+FP8X4 = mybir.dt.float8_e4m3fn_x4
+FP4X4 = mybir.dt.float4_e2m1fn_x4
+ACT = mybir.ActivationFunctionType
+ALU = mybir.AluOpType
+
+P = 128
+PACK = 4
+K_PASS = P * PACK
+PASSES = K // K_PASS
+CHUNK = 512
+CHUNKS = S // CHUNK
+HALF = P3 // 2
+QUADRANTS = 4
+PER_COLUMN = 16
+
+
+def tile_list_teacher_post_scores_kernel(
+    tc, tab_words, tab_scales, offs, w1, pos1, pos2, pos3, pos4, pos5, pos6, gain, w4_words, w4_scales, vac, out
+):
+    nc = tc.nc
+    with ExitStack() as ctx:
+        keep = ctx.enter_context(tc.tile_pool(name="keep", bufs=1))
+        psum = ctx.enter_context(tc.psum_pool(name="psum", bufs=8))
+
+        def load_list(name, source):
+            tile = keep.tile(list(source.shape), U16, name=name)
+            nc.sync.dma_start(tile[:], source)
+            return tile
+
+        def entries(tile, start, count):
+            return tile[:, start // PER_COLUMN : (start + count) // PER_COLUMN]
+
+        def load_w1(a, queue):
+            raw = keep.tile([P, PACK, H], F32, name="raw", tag=f"w1_raw{a}")
+            queue.dma_start(raw[:], w1[a * K_PASS : (a + 1) * K_PASS, :].rearrange("(p j) r -> p j r", j=PACK))
+            return raw
+
+        def load_words(a):
+            words = keep.tile([P, T], I32, name=f"table_words{a}")
+            nc.sync.dma_start(words[:], tab_words[a].rearrange("p t i -> p (t i)").bitcast(I32))
+            return words
+
+        idx = load_list("idx", offs)
+        w1_raw = [load_w1(0, nc.sync)]
+        table_scales = keep.tile([P, T], U8, name="table_scales")
+        nc.vector.memset(table_scales[:].bitcast(I32), 0)
+        for q in range(QUADRANTS):
+            nc.sync.dma_start(
+                table_scales[32 * q : 32 * q + 4 * PASSES, :].bitcast(I32),
+                tab_scales[:, 4 * q : 4 * q + 4, :].bitcast(I32),
+            )
+        table_words = [load_words(0)]
+        w1_raw.append(load_w1(1, nc.sync))
+        table_words.append(load_words(1))
+        p1, p2, p3, p4, p5, p6 = [
+            load_list(f"p{i + 1}", source) for i, source in enumerate((pos1, pos2, pos3, pos4, pos5, pos6))
+        ]
+
+        picked_scales = keep.tile([P, S], U8, name="picked_scales", align_bytes=64)
+        nc.vector.tensor_copy(picked_scales[:], table_scales[:].indirect(idx[:]))
+        w1_codes, w1_planes, picked_words = [], [], []
+        for a in range(PASSES):
+            grouped = keep.tile([P, H * PACK], BF16, name="grouped", tag=f"w1_grouped{a}", align_bytes=64)
+            nc.scalar.copy(
+                grouped[:].rearrange("p (t m j) -> p m t j", t=PACK, j=PACK),
+                w1_raw[a][:].rearrange("p j (m t) -> p m t j", t=PACK),
+            )
+            codes = keep.tile([P, H], U32, name=f"w1_codes{a}", align_bytes=64)
+            plane = keep.tile([P, H], U8, name=f"w1_plane{a}", align_bytes=64)
+            nc.vector.quantize_mx(out=codes[:].bitcast(FP8X4), scales=plane[:], in_=grouped[:])
+            w1_codes.append(codes)
+            w1_planes.append(plane)
+            picked = keep.tile([P, S], U32, name=f"picked_words{a}", align_bytes=64)
+            step = S if a < PASSES - 1 else CHUNK
+            for start in range(0, S, step):
+                nc.vector.tensor_copy(
+                    picked[:, start : start + step],
+                    table_words[a][:].bitcast(U32).indirect(entries(idx, start, step)),
+                )
+            picked_words.append(picked)
+
+        gains = keep.tile([P, PACK], F32, name="gains", tag="w1_raw1")
+        nc.sync.dma_start(gains[:], gain.rearrange("(p t) -> p t", t=PACK))
+        w4_codes = keep.tile([P, 2 * N], U8, name="w4_codes", tag="w1_grouped0", align_bytes=64)
+        nc.sync.dma_start(w4_codes[:].bitcast(I32), w4_words[0].bitcast(I32))
+        w4_plane = keep.tile([P, N], U8, name="w4_plane", tag="w1_grouped1", align_bytes=64)
+        nc.gpsimd.memset(w4_plane[:].bitcast(I32), 0)
+        for q in range(QUADRANTS):
+            nc.sync.dma_start(
+                w4_plane[32 * q : 32 * q + 4, :].bitcast(I32), w4_scales[0, 4 * q : 4 * q + 4, :].bitcast(I32)
+            )
+        vacancy = keep.tile([P, N // P, P3], F32, name="vacancy", tag="w1_raw0")
+        nc.sync.dma_start(vacancy[:], vac.rearrange("(b p) j -> p b j", p=P))
+
+        def first_pass(acc, t, c, a):
+            rows = slice(t * P, (t + 1) * P)
+            cols = slice(c * CHUNK, (c + 1) * CHUNK)
+            nc.tensor.matmul_mx(
+                out=acc[:],
+                lhsT=w1_codes[a][:, rows].bitcast(FP8X4),
+                lhsT_scale=w1_planes[a][:, rows],
+                rhs=picked_words[a][:, cols].bitcast(FP8X4),
+                rhs_scale=picked_scales[4 * a : P, cols],
+                start=(a == 0),
+                stop=(a == PASSES - 1),
+            )
+
+        def magnitude_tag(t, c):
+            if c == CHUNKS - 1:
+                return f"round{t}"
+            if t == PACK - 1 and c >= 1:
+                return f"grouped_half{c - 1}"
+            return f"magnitude{c}"
+
+        h = []
+        for t in range(PACK):
+            features = keep.tile([P, S], F32, name=f"h{t}")
+            sums = [psum.tile([P, CHUNK], F32, name="acc", tag="acc") for c in range(CHUNKS)]
+            for c in range(CHUNKS):
+                first_pass(sums[c], t, c, 0)
+            for c in range(CHUNKS):
+                first_pass(sums[c], t, c, 1)
+                magnitude = keep.tile([P, CHUNK], F32, name="magnitude", tag=magnitude_tag(t, c), align_bytes=64)
+                nc.scalar.activation(magnitude[:], sums[c][:], ACT.Abs)
+                nc.scalar.activation(
+                    features[:, c * CHUNK : (c + 1) * CHUNK], magnitude[:], ACT.Sin, bias=math.pi / 2, scale=-1.0
+                )
+            h.append(features)
+
+        a1 = [keep.tile([P, P1], F32, name=f"a1_{t}") for t in range(PACK)]
+        a2 = [keep.tile([P, P2], F32, name=f"a2_{t}") for t in range(PACK)]
+        larger = [keep.tile([P, P3], F32, name=f"larger{t}") for t in range(PACK)]
+        left1 = [keep.tile([P, P1], F32, name=f"left1_{t}") for t in range(PACK)]
+        grouped_a3 = [
+            keep.tile([P, HALF, PACK], BF16, name="grouped_a3", tag=f"grouped_half{u}", align_bytes=64)
+            for u in range(2)
+        ]
+        picks = [
+            keep.tile([P, P2 + 2 * P3], F32, name="picks", tag=f"round{r}", align_bytes=64)
+            for r in range(1, PACK + 2)
+        ]
+
+        def left2(t):
+            return picks[t][:, 0:P2]
+
+        def left3(t):
+            return picks[t + 1][:, P2 : P2 + P3]
+
+        def right3(t):
+            return picks[t + 1][:, P2 + P3 : P2 + 2 * P3]
+
+        def pick1(t, start=0, count=P1):
+            nc.vector.tensor_copy(left1[t][:, start : start + count], h[t][:].indirect(entries(p1, start, count)))
+
+        def multiply1(t, start=0, count=P1):
+            cols = slice(start, start + count)
+            nc.vector.tensor_tensor(
+                a1[t][:, cols], h[t][:].indirect(entries(p2, start, count)), left1[t][:, cols], ALU.mult
+            )
+
+        def pick2(t):
+            nc.vector.tensor_copy(left2(t), a1[t][:].indirect(p3[:]))
+
+        def add2(t):
+            nc.vector.tensor_tensor(a2[t][:], a1[t][:].indirect(p4[:]), left2(t), ALU.add)
+
+        def pick3_left(t, start=0, count=P3):
+            nc.vector.tensor_copy(left3(t)[:, start : start + count], a2[t][:].indirect(entries(p5, start, count)))
+
+        def pick3_right(t, start=0, count=P3):
+            nc.vector.tensor_copy(right3(t)[:, start : start + count], a2[t][:].indirect(entries(p6, start, count)))
+
+        def larger3(t, start=0, count=P3):
+            cols = slice(start, start + count)
+            nc.vector.tensor_tensor(larger[t][:, cols], left3(t)[:, cols], right3(t)[:, cols], ALU.max)
+
+        def round_a3(t, u):
+            nc.scalar.activation(
+                grouped_a3[u][:, :, t], larger[t][:, u * HALF : (u + 1) * HALF], ACT.Copy, scale=gains[:, t : t + 1]
+            )
+
+        def quantise_a3(u):
+            codes = keep.tile([P, HALF], U32, name=f"a3_codes{u}", align_bytes=64)
+            plane = keep.tile([P, HALF], U8, name=f"a3_plane{u}", align_bytes=64)
+            nc.vector.quantize_mx(
+                out=codes[:].bitcast(FP8X4), scales=plane[:], in_=grouped_a3[u][:].rearrange("p j t -> p (j t)")
+            )
+            return codes, plane
+
+        def scores(u, codes, plane):
+            cols = slice(u * HALF, (u + 1) * HALF)
+            y = psum.tile([P, N // P, HALF], F32, name="acc", tag="acc")
+            for b in range(N // P):
+                nc.tensor.matmul_mx(
+                    out=y[:, b, :],
+                    lhsT=w4_codes[:, 2 * b * P : 2 * (b + 1) * P].bitcast(FP4X4),
+                    lhsT_scale=w4_plane[:, b * P : (b + 1) * P],
+                    rhs=codes[:].bitcast(FP8X4),
+                    rhs_scale=plane[:],
+                    start=True,
+                    stop=True,
+                )
+            bounded = keep.tile([P, N // P, HALF], F32, name=f"bounded{u}")
+            nc.scalar.activation(bounded[:], y[:], ACT.Tanh)
+            result = keep.tile([P, N // P, HALF], F32, name=f"result{u}")
+            nc.vector.tensor_tensor(result[:], bounded[:], vacancy[:, :, cols], ALU.mult)
+            nc.sync.dma_start(out.rearrange("(b p) j -> p b j", p=P)[:, :, cols], result[:])
+
+        for start in (0, P1 // 2):
+            pick1(0, start, P1 // 2)
+        for start in (0, P1 // 2):
+            multiply1(0, start, P1 // 2)
+        for r in range(1, PACK):
+            pick1(r)
+            if r >= 2:
+                pick3_left(r - 2)
+                pick3_right(r - 2)
+            pick2(r - 1)
+            if r >= 2:
+                larger3(r - 2)
+            multiply1(r)
+            add2(r - 1)
+        last = PACK - 1
+        pick2(last)
+        pick3_left(last - 1)
+        add2(last)
+        pick3_right(last - 1)
+        pick3_left(last, 0, HALF)
+        larger3(last - 1)
+        for t in range(last):
+            for u in range(2):
+                round_a3(t, u)
+        pick3_right(last, 0, HALF)
+        pick3_left(last, HALF, HALF)
+        larger3(last, 0, HALF)
+        round_a3(last, 0)
+        pick3_right(last, HALF, HALF)
+        larger3(last, HALF, HALF)
+        round_a3(last, 1)
+        quantised = [quantise_a3(u) for u in range(2)]
+        for u in range(2):
+            scores(u, *quantised[u])

@@ -44,6 +44,11 @@ def tile_list_teacher_post_scores_kernel(
         def entries(tile, start, count):
             return tile[:, start // PER_COLUMN : (start + count) // PER_COLUMN]
 
+        warm_in = keep.tile([P, 1], F32, name="warm_in")
+        warm_out = keep.tile([P, 1], F32, name="warm_out")
+        nc.gpsimd.memset(warm_in[:], 0.0)
+        nc.scalar.activation(warm_out[:], warm_in[:], ACT.Silu)
+
         def load_w1(a, queue):
             raw = keep.tile([P, PACK, H], F32, name="raw", tag=f"w1_raw{a}")
             queue.dma_start(raw[:], w1[a * K_PASS : (a + 1) * K_PASS, :].rearrange("(p j) r -> p j r", j=PACK))

@@ -49,18 +49,19 @@ def tile_list_teacher_post_scores_kernel(
         nc.gpsimd.memset(warm_in[:], 0.0)
         nc.scalar.activation(warm_out[:], warm_in[:], ACT.Silu)
 
-        def load_w1(a, queue):
-            raw = keep.tile([P, PACK, H], F32, name="raw", tag=f"w1_raw{a}")
-            queue.dma_start(raw[:], w1[a * K_PASS : (a + 1) * K_PASS, :].rearrange("(p j) r -> p j r", j=PACK))
-            return raw
+        def load_w1(a, start, count):
+            raw = keep.tile([P, PACK, count], F32, name="raw", tag=f"w1_raw{a}_{start}")
+            rows = w1[a * K_PASS : (a + 1) * K_PASS, start : start + count]
+            nc.sync.dma_start(raw[:], rows.rearrange("(p j) r -> p j r", j=PACK))
+            return a, start, count, raw
 
         def load_words(a):
-            words = keep.tile([P, T], I32, name=f"table_words{a}")
+            words = keep.tile([P, T], I32, name="words", tag=f"table_words{a}", align_bytes=64)
             nc.sync.dma_start(words[:], tab_words[a].rearrange("p t i -> p (t i)").bitcast(I32))
             return words
 
         idx = load_list("idx", offs)
-        w1_raw = [load_w1(0, nc.sync)]
+        w1_parts = [load_w1(0, 0, H)]
         table_scales = keep.tile([P, T], U8, name="table_scales")
         nc.vector.memset(table_scales[:].bitcast(I32), 0)
         for q in range(QUADRANTS):
@@ -68,8 +69,9 @@ def tile_list_teacher_post_scores_kernel(
                 table_scales[32 * q : 32 * q + 4 * PASSES, :].bitcast(I32),
                 tab_scales[:, 4 * q : 4 * q + 4, :].bitcast(I32),
             )
+        w1_parts.append(load_w1(1, 0, H // 2))
         table_words = [load_words(0)]
-        w1_raw.append(load_w1(1, nc.sync))
+        w1_parts.append(load_w1(1, H // 2, H // 2))
         table_words.append(load_words(1))
         p1, p2, p3, p4, p5, p6 = [
             load_list(f"p{i + 1}", source) for i, source in enumerate((pos1, pos2, pos3, pos4, pos5, pos6))
@@ -77,18 +79,24 @@ def tile_list_teacher_post_scores_kernel(
 
         picked_scales = keep.tile([P, S], U8, name="picked_scales", align_bytes=64)
         nc.vector.tensor_copy(picked_scales[:], table_scales[:].indirect(idx[:]))
-        w1_codes, w1_planes, picked_words = [], [], []
-        for a in range(PASSES):
-            grouped = keep.tile([P, H * PACK], BF16, name="grouped", tag=f"w1_grouped{a}", align_bytes=64)
+        w1_grouped = [
+            keep.tile([P, H * PACK], BF16, name="grouped", tag=f"w1_grouped{a}", align_bytes=64)
+            for a in range(PASSES)
+        ]
+        for a, start, count, raw in w1_parts:
             nc.scalar.copy(
-                grouped[:].rearrange("p (t m j) -> p m t j", t=PACK, j=PACK),
-                w1_raw[a][:].rearrange("p j (m t) -> p m t j", t=PACK),
+                w1_grouped[a][:].rearrange("p (t m j) -> p m t j", t=PACK, j=PACK)[
+                    :, start // PACK : (start + count) // PACK
+                ],
+                raw[:].rearrange("p j (m t) -> p m t j", t=PACK),
             )
-            codes = keep.tile([P, H], U32, name=f"w1_codes{a}", align_bytes=64)
-            plane = keep.tile([P, H], U8, name=f"w1_plane{a}", align_bytes=64)
-            nc.vector.quantize_mx(out=codes[:].bitcast(FP8X4), scales=plane[:], in_=grouped[:])
-            w1_codes.append(codes)
-            w1_planes.append(plane)
+        w1_planes = keep.tile([P, PASSES, H], U8, name="w1_planes", align_bytes=64)
+        first_codes = keep.tile([P, PASSES, P], U32, name="first_codes", align_bytes=64)
+        picked_words = []
+        for a in range(PASSES):
+            nc.vector.quantize_mx(
+                out=first_codes[:, a, :].bitcast(FP8X4), scales=w1_planes[:, a, 0:P], in_=w1_grouped[a][:, 0:K_PASS]
+            )
             picked = keep.tile([P, S], U32, name=f"picked_words{a}", align_bytes=64)
             step = S if a < PASSES - 1 else CHUNK
             for start in range(0, S, step):
@@ -97,8 +105,18 @@ def tile_list_teacher_post_scores_kernel(
                     table_words[a][:].bitcast(U32).indirect(entries(idx, start, step)),
                 )
             picked_words.append(picked)
+        later_codes = keep.tile([P, PASSES, H - P], U32, name="later_codes", tag="table_words1", align_bytes=64)
+        for a in range(PASSES):
+            nc.vector.quantize_mx(
+                out=later_codes[:, a, :].bitcast(FP8X4),
+                scales=w1_planes[:, a, P:H],
+                in_=w1_grouped[a][:, K_PASS : H * PACK],
+            )
 
-        gains = keep.tile([P, PACK], F32, name="gains", tag="w1_raw1")
+        def w1_codes(a, t):
+            return first_codes[:, a, :] if t == 0 else later_codes[:, a, (t - 1) * P : t * P]
+
+        gains = keep.tile([P, PACK], F32, name="gains", tag="w1_raw1_0")
         nc.sync.dma_start(gains[:], gain.rearrange("(p t) -> p t", t=PACK))
         w4_codes = keep.tile([P, 2 * N], U8, name="w4_codes", tag="w1_grouped0", align_bytes=64)
         nc.sync.dma_start(w4_codes[:].bitcast(I32), w4_words[0].bitcast(I32))
@@ -108,42 +126,45 @@ def tile_list_teacher_post_scores_kernel(
             nc.sync.dma_start(
                 w4_plane[32 * q : 32 * q + 4, :].bitcast(I32), w4_scales[0, 4 * q : 4 * q + 4, :].bitcast(I32)
             )
-        vacancy = keep.tile([P, N // P, P3], F32, name="vacancy", tag="w1_raw0")
+        vacancy = keep.tile([P, N // P, P3], F32, name="vacancy", tag="w1_raw0_0")
         nc.sync.dma_start(vacancy[:], vac.rearrange("(b p) j -> p b j", p=P))
 
-        def first_pass(acc, t, c, a):
-            rows = slice(t * P, (t + 1) * P)
-            cols = slice(c * CHUNK, (c + 1) * CHUNK)
+        def first_pass(acc, t, cols, a):
             nc.tensor.matmul_mx(
                 out=acc[:],
-                lhsT=w1_codes[a][:, rows].bitcast(FP8X4),
-                lhsT_scale=w1_planes[a][:, rows],
+                lhsT=w1_codes(a, t).bitcast(FP8X4),
+                lhsT_scale=w1_planes[:, a, t * P : (t + 1) * P],
                 rhs=picked_words[a][:, cols].bitcast(FP8X4),
                 rhs_scale=picked_scales[4 * a : P, cols],
                 start=(a == 0),
                 stop=(a == PASSES - 1),
             )
 
-        def magnitude_tag(t, c):
-            if c == CHUNKS - 1:
+        def magnitude_tag(t, c, count):
+            if c == count - 1:
                 return f"round{t}"
             if t == PACK - 1 and c >= 1:
                 return f"grouped_half{c - 1}"
-            return f"magnitude{c}"
+            return f"magnitude{c % 4}"
 
         h = []
         for t in range(PACK):
+            width = CHUNK // 2 if t == 0 else CHUNK
+            chunks = [slice(start, start + width) for start in range(0, S, width)]
             features = keep.tile([P, S], F32, name=f"h{t}")
-            sums = [psum.tile([P, CHUNK], F32, name="acc", tag="acc") for c in range(CHUNKS)]
-            for c in range(CHUNKS):
-                first_pass(sums[c], t, c, 0)
-            for c in range(CHUNKS):
-                first_pass(sums[c], t, c, 1)
-                magnitude = keep.tile([P, CHUNK], F32, name="magnitude", tag=magnitude_tag(t, c), align_bytes=64)
-                nc.scalar.activation(magnitude[:], sums[c][:], ACT.Abs)
-                nc.scalar.activation(
-                    features[:, c * CHUNK : (c + 1) * CHUNK], magnitude[:], ACT.Sin, bias=math.pi / 2, scale=-1.0
-                )
+            sums = [psum.tile([P, width], F32, name="acc", tag="acc") for cols in chunks]
+            for acc, cols in zip(sums, chunks):
+                first_pass(acc, t, cols, 0)
+            for pair in range(0, len(chunks), 2):
+                magnitudes = []
+                for c in (pair, pair + 1):
+                    first_pass(sums[c], t, chunks[c], 1)
+                    tag = magnitude_tag(t, c, len(chunks))
+                    magnitude = keep.tile([P, width], F32, name="magnitude", tag=tag, align_bytes=64)
+                    nc.scalar.activation(magnitude[:], sums[c][:], ACT.Abs)
+                    magnitudes.append(magnitude)
+                for c, magnitude in zip((pair, pair + 1), magnitudes):
+                    nc.scalar.activation(features[:, chunks[c]], magnitude[:], ACT.Sin, bias=math.pi / 2, scale=-1.0)
             h.append(features)
 
         a1 = [keep.tile([P, P1], F32, name=f"a1_{t}") for t in range(PACK)]
@@ -206,12 +227,14 @@ def tile_list_teacher_post_scores_kernel(
             )
             return codes, plane
 
-        def scores(u, codes, plane):
+        def scores(u, codes, plane, first, count):
             cols = slice(u * HALF, (u + 1) * HALF)
-            y = psum.tile([P, N // P, HALF], F32, name="acc", tag="acc")
-            for b in range(N // P):
+            blocks = slice(first, first + count)
+            y = psum.tile([P, count, HALF], F32, name="acc", tag="acc")
+            for i in range(count):
+                b = first + i
                 nc.tensor.matmul_mx(
-                    out=y[:, b, :],
+                    out=y[:, i, :],
                     lhsT=w4_codes[:, 2 * b * P : 2 * (b + 1) * P].bitcast(FP4X4),
                     lhsT_scale=w4_plane[:, b * P : (b + 1) * P],
                     rhs=codes[:].bitcast(FP8X4),
@@ -219,11 +242,11 @@ def tile_list_teacher_post_scores_kernel(
                     start=True,
                     stop=True,
                 )
-            bounded = keep.tile([P, N // P, HALF], F32, name=f"bounded{u}")
+            bounded = keep.tile([P, count, HALF], F32, name=f"bounded{u}_{first}")
             nc.scalar.activation(bounded[:], y[:], ACT.Tanh)
-            result = keep.tile([P, N // P, HALF], F32, name=f"result{u}")
-            nc.vector.tensor_tensor(result[:], bounded[:], vacancy[:, :, cols], ALU.mult)
-            nc.sync.dma_start(out.rearrange("(b p) j -> p b j", p=P)[:, :, cols], result[:])
+            result = keep.tile([P, count, HALF], F32, name=f"result{u}_{first}")
+            nc.vector.tensor_tensor(result[:], bounded[:], vacancy[:, blocks, cols], ALU.mult)
+            nc.sync.dma_start(out.rearrange("(b p) j -> p b j", p=P)[:, blocks, cols], result[:])
 
         for start in (0, P1 // 2):
             pick1(0, start, P1 // 2)
@@ -242,13 +265,13 @@ def tile_list_teacher_post_scores_kernel(
         last = PACK - 1
         pick2(last)
         pick3_left(last - 1)
-        add2(last)
         pick3_right(last - 1)
-        pick3_left(last, 0, HALF)
+        add2(last)
         larger3(last - 1)
         for t in range(last):
             for u in range(2):
                 round_a3(t, u)
+        pick3_left(last, 0, HALF)
         pick3_right(last, 0, HALF)
         pick3_left(last, HALF, HALF)
         larger3(last, 0, HALF)
@@ -258,4 +281,5 @@ def tile_list_teacher_post_scores_kernel(
         round_a3(last, 1)
         quantised = [quantise_a3(u) for u in range(2)]
         for u in range(2):
-            scores(u, *quantised[u])
+            for first in (0, 2):
+                scores(u, *quantised[u], first, 2)

@@ -49,11 +49,11 @@ def tile_list_teacher_post_scores_kernel(
         nc.gpsimd.memset(warm_in[:], 0.0)
         nc.scalar.activation(warm_out[:], warm_in[:], ACT.Silu)
 
-        def load_w1(a, start, count):
-            raw = keep.tile([P, PACK, count], F32, name="raw", tag=f"w1_raw{a}_{start}")
-            rows = w1[a * K_PASS : (a + 1) * K_PASS, start : start + count]
-            nc.sync.dma_start(raw[:], rows.rearrange("(p j) r -> p j r", j=PACK))
-            return a, start, count, raw
+        w1_raw = [keep.tile([P, PACK, H], F32, name="raw", tag=f"w1_raw{a}_0") for a in range(PASSES)]
+
+        def load_w1(a, first, count):
+            rows = w1[a * K_PASS : (a + 1) * K_PASS, :].rearrange("(p j) r -> p j r", j=PACK)
+            nc.sync.dma_start(w1_raw[a][:, first : first + count, :], rows[:, first : first + count, :])
 
         def load_words(a):
             words = keep.tile([P, T], I32, name="words", tag=f"table_words{a}", align_bytes=64)
@@ -61,7 +61,7 @@ def tile_list_teacher_post_scores_kernel(
             return words
 
         idx = load_list("idx", offs)
-        w1_parts = [load_w1(0, 0, H)]
+        load_w1(0, 0, 2)
         table_scales = keep.tile([P, T], U8, name="table_scales")
         nc.vector.memset(table_scales[:].bitcast(I32), 0)
         for q in range(QUADRANTS):
@@ -69,9 +69,9 @@ def tile_list_teacher_post_scores_kernel(
                 table_scales[32 * q : 32 * q + 4 * PASSES, :].bitcast(I32),
                 tab_scales[:, 4 * q : 4 * q + 4, :].bitcast(I32),
             )
-        w1_parts.append(load_w1(1, 0, H // 2))
+        load_w1(0, 2, 2)
         table_words = [load_words(0)]
-        w1_parts.append(load_w1(1, H // 2, H // 2))
+        load_w1(1, 0, PACK)
         table_words.append(load_words(1))
         p1, p2, p3, p4, p5, p6 = [
             load_list(f"p{i + 1}", source) for i, source in enumerate((pos1, pos2, pos3, pos4, pos5, pos6))
@@ -83,12 +83,10 @@ def tile_list_teacher_post_scores_kernel(
             keep.tile([P, H * PACK], BF16, name="grouped", tag=f"w1_grouped{a}", align_bytes=64)
             for a in range(PASSES)
         ]
-        for a, start, count, raw in w1_parts:
+        for a in range(PASSES):
             nc.scalar.copy(
-                w1_grouped[a][:].rearrange("p (t m j) -> p m t j", t=PACK, j=PACK)[
-                    :, start // PACK : (start + count) // PACK
-                ],
-                raw[:].rearrange("p j (m t) -> p m t j", t=PACK),
+                w1_grouped[a][:].rearrange("p (t m j) -> p m t j", t=PACK, j=PACK),
+                w1_raw[a][:].rearrange("p j (m t) -> p m t j", t=PACK),
             )
         w1_planes = keep.tile([P, PASSES, H], U8, name="w1_planes", align_bytes=64)
         first_codes = keep.tile([P, PASSES, P], U32, name="first_codes", align_bytes=64)
@@ -98,7 +96,7 @@ def tile_list_teacher_post_scores_kernel(
                 out=first_codes[:, a, :].bitcast(FP8X4), scales=w1_planes[:, a, 0:P], in_=w1_grouped[a][:, 0:K_PASS]
             )
             picked = keep.tile([P, S], U32, name=f"picked_words{a}", align_bytes=64)
-            step = S if a < PASSES - 1 else CHUNK
+            step = S // 2 if a < PASSES - 1 else CHUNK
             for start in range(0, S, step):
                 nc.vector.tensor_copy(
                     picked[:, start : start + step],
@@ -106,12 +104,13 @@ def tile_list_teacher_post_scores_kernel(
                 )
             picked_words.append(picked)
         later_codes = keep.tile([P, PASSES, H - P], U32, name="later_codes", tag="table_words1", align_bytes=64)
-        for a in range(PASSES):
-            nc.vector.quantize_mx(
-                out=later_codes[:, a, :].bitcast(FP8X4),
-                scales=w1_planes[:, a, P:H],
-                in_=w1_grouped[a][:, K_PASS : H * PACK],
-            )
+        for start, stop in ((P, 2 * P), (2 * P, H)):
+            for a in range(PASSES):
+                nc.vector.quantize_mx(
+                    out=later_codes[:, a, start - P : stop - P].bitcast(FP8X4),
+                    scales=w1_planes[:, a, start:stop],
+                    in_=w1_grouped[a][:, start * PACK : stop * PACK],
+                )
 
         def w1_codes(a, t):
             return first_codes[:, a, :] if t == 0 else later_codes[:, a, (t - 1) * P : t * P]
@@ -153,12 +152,14 @@ def tile_list_teacher_post_scores_kernel(
             chunks = [slice(start, start + width) for start in range(0, S, width)]
             features = keep.tile([P, S], F32, name=f"h{t}")
             sums = [psum.tile([P, width], F32, name="acc", tag="acc") for cols in chunks]
-            for acc, cols in zip(sums, chunks):
-                first_pass(acc, t, cols, 0)
+            if t == 0:
+                for acc, cols in zip(sums, chunks):
+                    first_pass(acc, t, cols, 0)
             for pair in range(0, len(chunks), 2):
                 magnitudes = []
                 for c in (pair, pair + 1):
-                    first_pass(sums[c], t, chunks[c], 1)
+                    for a in range(1 if t == 0 else 0, PASSES):
+                        first_pass(sums[c], t, chunks[c], a)
                     tag = magnitude_tag(t, c, len(chunks))
                     magnitude = keep.tile([P, width], F32, name="magnitude", tag=tag, align_bytes=64)
                     nc.scalar.activation(magnitude[:], sums[c][:], ACT.Abs)

@@ -170,7 +170,7 @@ def tile_list_teacher_post_scores_kernel(
 
         a1 = [keep.tile([P, P1], F32, name=f"a1_{t}") for t in range(PACK)]
         a2 = [keep.tile([P, P2], F32, name=f"a2_{t}") for t in range(PACK)]
-        larger = [keep.tile([P, P3], F32, name=f"larger{t}") for t in range(PACK)]
+        larger = [keep.tile([P, P3], F32, name=f"larger{t}") for t in range(2)]
         left1 = [keep.tile([P, P1], F32, name=f"left1_{t}") for t in range(PACK)]
         grouped_a3 = [
             keep.tile([P, HALF, PACK], BF16, name="grouped_a3", tag=f"grouped_half{u}", align_bytes=64)
@@ -178,7 +178,7 @@ def tile_list_teacher_post_scores_kernel(
         ]
         picks = [
             keep.tile([P, P2 + 2 * P3], F32, name="picks", tag=f"round{r}", align_bytes=64)
-            for r in range(1, PACK + 2)
+            for r in range(1, PACK + 1)
         ]
 
         def left2(t):
@@ -214,6 +214,24 @@ def tile_list_teacher_post_scores_kernel(
         def larger3(t, start=0, count=P3):
             cols = slice(start, start + count)
             nc.vector.tensor_tensor(larger[t][:, cols], left3(t)[:, cols], right3(t)[:, cols], ALU.max)
+
+        late_gains = keep.tile([P, 2, HALF], F32, name="late_gains", tag="magnitude0", align_bytes=64)
+        nc.scalar.copy(late_gains[:], gains[:, 2:PACK].unsqueeze(2).to_broadcast([P, 2, HALF]))
+        late_picks = [keep.tile([P, 2, P3], F32, name=f"late_picks{side}") for side in range(2)]
+
+        def pick3_late(t, side, u):
+            nc.vector.tensor_tensor(
+                late_picks[side][:, t - 2, u * HALF : (u + 1) * HALF],
+                a2[t][:].indirect(entries((p5, p6)[side], u * HALF, HALF)),
+                late_gains[:, t - 2, :],
+                ALU.mult,
+            )
+
+        def larger3_late(u):
+            left, right = [
+                tile[:, :, u * HALF : (u + 1) * HALF].rearrange("p t j -> p j t") for tile in late_picks
+            ]
+            nc.vector.tensor_tensor(grouped_a3[u][:, :, 2:PACK], left, right, ALU.max)
 
         def round_a3(t, u):
             nc.scalar.activation(
@@ -263,24 +281,23 @@ def tile_list_teacher_post_scores_kernel(
                 larger3(r - 2)
             multiply1(r)
             add2(r - 1)
-        last = PACK - 1
-        pick2(last)
-        pick3_left(last - 1)
-        pick3_right(last - 1)
-        add2(last)
-        larger3(last - 1)
-        for t in range(last):
+        for t in range(2):
             for u in range(2):
                 round_a3(t, u)
-        pick3_left(last, 0, HALF)
-        pick3_right(last, 0, HALF)
-        pick3_left(last, HALF, HALF)
-        larger3(last, 0, HALF)
-        round_a3(last, 0)
-        pick3_right(last, HALF, HALF)
-        larger3(last, HALF, HALF)
-        round_a3(last, 1)
-        quantised = [quantise_a3(u) for u in range(2)]
+        pick2(3)
+        pick3_late(2, 0, 0)
+        pick3_late(2, 1, 0)
+        add2(3)
+        pick3_late(2, 0, 1)
+        pick3_late(2, 1, 1)
+        pick3_late(3, 0, 0)
+        pick3_late(3, 1, 0)
+        pick3_late(3, 0, 1)
+        larger3_late(0)
+        pick3_late(3, 1, 1)
+        quantised = [quantise_a3(0)]
+        larger3_late(1)
+        quantised.append(quantise_a3(1))
         for u in range(2):
             for first in (0, 2):
                 scores(u, *quantised[u], first, 2)

import math
from contextlib import ExitStack

import concourse.mybir as mybir

K, T, S, H, N, P1, P2, P3 = 1024, 4096, 2048, 512, 512, 1024, 512, 256
FLOPS = 2 * K * H * S + 2 * H * N * P3

F32 = mybir.dt.float32
BF16 = mybir.dt.bfloat16
I32 = mybir.dt.int32
U32 = mybir.dt.uint32
U16 = mybir.dt.uint16
U8 = mybir.dt.uint8
FP8X4 = mybir.dt.float8_e4m3fn_x4
FP4X4 = mybir.dt.float4_e2m1fn_x4
ACT = mybir.ActivationFunctionType
ALU = mybir.AluOpType

P = 128
PACK = 4
K_PASS = P * PACK
PASSES = K // K_PASS
CHUNK = 512
CHUNKS = S // CHUNK
HALF = P3 // 2
QUADRANTS = 4
PER_COLUMN = 16


def tile_list_teacher_post_scores_kernel(
    tc, tab_words, tab_scales, offs, w1, pos1, pos2, pos3, pos4, pos5, pos6, gain, w4_words, w4_scales, vac, out
):
    nc = tc.nc
    with ExitStack() as ctx:
        keep = ctx.enter_context(tc.tile_pool(name="keep", bufs=1))
        psum = ctx.enter_context(tc.psum_pool(name="psum", bufs=8))

        def load_list(name, source):
            tile = keep.tile(list(source.shape), U16, name=name)
            nc.sync.dma_start(tile[:], source)
            return tile

        def entries(tile, start, count):
            return tile[:, start // PER_COLUMN : (start + count) // PER_COLUMN]

        warm_in = keep.tile([P, 1], F32, name="warm_in")
        warm_out = keep.tile([P, 1], F32, name="warm_out")
        nc.gpsimd.memset(warm_in[:], 0.0)
        nc.scalar.activation(warm_out[:], warm_in[:], ACT.Silu)

        w1_raw = [keep.tile([P, PACK, H], F32, name="raw", tag=f"w1_raw{a}_0") for a in range(PASSES)]

        def load_w1(a, first, count):
            rows = w1[a * K_PASS : (a + 1) * K_PASS, :].rearrange("(p j) r -> p j r", j=PACK)
            nc.sync.dma_start(w1_raw[a][:, first : first + count, :], rows[:, first : first + count, :])

        def load_words(a):
            words = keep.tile([P, T], I32, name="words", tag=f"table_words{a}", align_bytes=64)
            nc.sync.dma_start(words[:], tab_words[a].rearrange("p t i -> p (t i)").bitcast(I32))
            return words

        idx = load_list("idx", offs)
        load_w1(0, 0, 2)
        table_scales = keep.tile([P, T], U8, name="table_scales")
        nc.vector.memset(table_scales[:].bitcast(I32), 0)
        for q in range(QUADRANTS):
            nc.sync.dma_start(
                table_scales[32 * q : 32 * q + 4 * PASSES, :].bitcast(I32),
                tab_scales[:, 4 * q : 4 * q + 4, :].bitcast(I32),
            )
        load_w1(0, 2, 2)
        table_words = [load_words(0)]
        load_w1(1, 0, PACK)
        table_words.append(load_words(1))
        p1, p2, p3, p4, p5, p6 = [
            load_list(f"p{i + 1}", source) for i, source in enumerate((pos1, pos2, pos3, pos4, pos5, pos6))
        ]

        picked_scales = keep.tile([P, S], U8, name="picked_scales", align_bytes=64)
        nc.vector.tensor_copy(picked_scales[:], table_scales[:].indirect(idx[:]))
        w1_grouped = [
            keep.tile([P, H * PACK], BF16, name="grouped", tag=f"w1_grouped{a}", align_bytes=64)
            for a in range(PASSES)
        ]
        for a in range(PASSES):
            nc.scalar.copy(
                w1_grouped[a][:].rearrange("p (t m j) -> p m t j", t=PACK, j=PACK),
                w1_raw[a][:].rearrange("p j (m t) -> p m t j", t=PACK),
            )
        w1_planes = keep.tile([P, PASSES, H], U8, name="w1_planes", align_bytes=64)
        first_codes = keep.tile([P, PASSES, P], U32, name="first_codes", align_bytes=64)
        picked_words = []
        for a in range(PASSES):
            nc.vector.quantize_mx(
                out=first_codes[:, a, :].bitcast(FP8X4), scales=w1_planes[:, a, 0:P], in_=w1_grouped[a][:, 0:K_PASS]
            )
            picked = keep.tile([P, S], U32, name=f"picked_words{a}", align_bytes=64)
            step = S // 2 if a < PASSES - 1 else CHUNK
            for start in range(0, S, step):
                nc.vector.tensor_copy(
                    picked[:, start : start + step],
                    table_words[a][:].bitcast(U32).indirect(entries(idx, start, step)),
                )
            picked_words.append(picked)
        later_codes = keep.tile([P, PASSES, H - P], U32, name="later_codes", tag="table_words1", align_bytes=64)
        for start, stop in ((P, 2 * P), (2 * P, H)):
            for a in range(PASSES):
                nc.vector.quantize_mx(
                    out=later_codes[:, a, start - P : stop - P].bitcast(FP8X4),
                    scales=w1_planes[:, a, start:stop],
                    in_=w1_grouped[a][:, start * PACK : stop * PACK],
                )

        def w1_codes(a, t):
            return first_codes[:, a, :] if t == 0 else later_codes[:, a, (t - 1) * P : t * P]

        gains = keep.tile([P, PACK], F32, name="gains", tag="w1_raw1_0")
        nc.sync.dma_start(gains[:], gain.rearrange("(p t) -> p t", t=PACK))
        w4_codes = keep.tile([P, 2 * N], U8, name="w4_codes", tag="w1_grouped0", align_bytes=64)
        nc.sync.dma_start(w4_codes[:].bitcast(I32), w4_words[0].bitcast(I32))
        w4_plane = keep.tile([P, N], U8, name="w4_plane", tag="w1_grouped1", align_bytes=64)
        nc.gpsimd.memset(w4_plane[:].bitcast(I32), 0)
        for q in range(QUADRANTS):
            nc.sync.dma_start(
                w4_plane[32 * q : 32 * q + 4, :].bitcast(I32), w4_scales[0, 4 * q : 4 * q + 4, :].bitcast(I32)
            )
        vacancy = keep.tile([P, N // P, P3], F32, name="vacancy", tag="w1_raw0_0")
        nc.sync.dma_start(vacancy[:], vac.rearrange("(b p) j -> p b j", p=P))

        def first_pass(acc, t, cols, a):
            nc.tensor.matmul_mx(
                out=acc[:],
                lhsT=w1_codes(a, t).bitcast(FP8X4),
                lhsT_scale=w1_planes[:, a, t * P : (t + 1) * P],
                rhs=picked_words[a][:, cols].bitcast(FP8X4),
                rhs_scale=picked_scales[4 * a : P, cols],
                start=(a == 0),
                stop=(a == PASSES - 1),
            )

        def magnitude_tag(t, c, count):
            if c == count - 1:
                return f"round{t}"
            if t == PACK - 1 and c >= 1:
                return f"grouped_half{c - 1}"
            return f"magnitude{c % 4}"

        h = []
        for t in range(PACK):
            width = CHUNK // 2 if t == 0 else CHUNK
            chunks = [slice(start, start + width) for start in range(0, S, width)]
            features = keep.tile([P, S], F32, name=f"h{t}")
            sums = [psum.tile([P, width], F32, name="acc", tag="acc") for cols in chunks]
            if t == 0:
                for acc, cols in zip(sums, chunks):
                    first_pass(acc, t, cols, 0)
            for pair in range(0, len(chunks), 2):
                magnitudes = []
                for c in (pair, pair + 1):
                    for a in range(1 if t == 0 else 0, PASSES):
                        first_pass(sums[c], t, chunks[c], a)
                    tag = magnitude_tag(t, c, len(chunks))
                    magnitude = keep.tile([P, width], F32, name="magnitude", tag=tag, align_bytes=64)
                    nc.scalar.activation(magnitude[:], sums[c][:], ACT.Abs)
                    magnitudes.append(magnitude)
                for c, magnitude in zip((pair, pair + 1), magnitudes):
                    nc.scalar.activation(features[:, chunks[c]], magnitude[:], ACT.Sin, bias=math.pi / 2, scale=-1.0)
            h.append(features)

        a1 = [keep.tile([P, P1], F32, name=f"a1_{t}") for t in range(PACK)]
        a2 = [keep.tile([P, P2], F32, name=f"a2_{t}") for t in range(PACK)]
        larger = [keep.tile([P, P3], F32, name=f"larger{t}") for t in range(2)]
        left1 = [keep.tile([P, P1], F32, name=f"left1_{t}") for t in range(PACK)]
        grouped_a3 = [
            keep.tile([P, HALF, PACK], BF16, name="grouped_a3", tag=f"grouped_half{u}", align_bytes=64)
            for u in range(2)
        ]
        picks = [
            keep.tile([P, P2 + 2 * P3], F32, name="picks", tag=f"round{r}", align_bytes=64)
            for r in range(1, PACK + 1)
        ]

        def left2(t):
            return picks[t][:, 0:P2]

        def left3(t):
            return picks[t + 1][:, P2 : P2 + P3]

        def right3(t):
            return picks[t + 1][:, P2 + P3 : P2 + 2 * P3]

        def pick1(t, start=0, count=P1):
            nc.vector.tensor_copy(left1[t][:, start : start + count], h[t][:].indirect(entries(p1, start, count)))

        def multiply1(t, start=0, count=P1):
            cols = slice(start, start + count)
            nc.vector.tensor_tensor(
                a1[t][:, cols], h[t][:].indirect(entries(p2, start, count)), left1[t][:, cols], ALU.mult
            )

        def pick2(t):
            nc.vector.tensor_copy(left2(t), a1[t][:].indirect(p3[:]))

        def add2(t):
            nc.vector.tensor_tensor(a2[t][:], a1[t][:].indirect(p4[:]), left2(t), ALU.add)

        def pick3_left(t, start=0, count=P3):
            nc.vector.tensor_copy(left3(t)[:, start : start + count], a2[t][:].indirect(entries(p5, start, count)))

        def pick3_right(t, start=0, count=P3):
            nc.vector.tensor_copy(right3(t)[:, start : start + count], a2[t][:].indirect(entries(p6, start, count)))

        def larger3(t, start=0, count=P3):
            cols = slice(start, start + count)
            nc.vector.tensor_tensor(larger[t][:, cols], left3(t)[:, cols], right3(t)[:, cols], ALU.max)

        late_gains = keep.tile([P, 2, HALF], F32, name="late_gains", tag="magnitude0", align_bytes=64)
        nc.scalar.copy(late_gains[:], gains[:, 2:PACK].unsqueeze(2).to_broadcast([P, 2, HALF]))
        late_picks = [keep.tile([P, 2, P3], F32, name=f"late_picks{side}") for side in range(2)]

        def pick3_late(t, side, u):
            nc.vector.tensor_tensor(
                late_picks[side][:, t - 2, u * HALF : (u + 1) * HALF],
                a2[t][:].indirect(entries((p5, p6)[side], u * HALF, HALF)),
                late_gains[:, t - 2, :],
                ALU.mult,
            )

        def larger3_late(u):
            left, right = [
                tile[:, :, u * HALF : (u + 1) * HALF].rearrange("p t j -> p j t") for tile in late_picks
            ]
            nc.vector.tensor_tensor(grouped_a3[u][:, :, 2:PACK], left, right, ALU.max)

        def round_a3(t, u):
            nc.scalar.activation(
                grouped_a3[u][:, :, t], larger[t][:, u * HALF : (u + 1) * HALF], ACT.Copy, scale=gains[:, t : t + 1]
            )

        def quantise_a3(u):
            codes = keep.tile([P, HALF], U32, name=f"a3_codes{u}", align_bytes=64)
            plane = keep.tile([P, HALF], U8, name=f"a3_plane{u}", align_bytes=64)
            nc.vector.quantize_mx(
                out=codes[:].bitcast(FP8X4), scales=plane[:], in_=grouped_a3[u][:].rearrange("p j t -> p (j t)")
            )
            return codes, plane

        def scores(u, codes, plane, first, count):
            cols = slice(u * HALF, (u + 1) * HALF)
            blocks = slice(first, first + count)
            y = psum.tile([P, count, HALF], F32, name="acc", tag="acc")
            for i in range(count):
                b = first + i
                nc.tensor.matmul_mx(
                    out=y[:, i, :],
                    lhsT=w4_codes[:, 2 * b * P : 2 * (b + 1) * P].bitcast(FP4X4),
                    lhsT_scale=w4_plane[:, b * P : (b + 1) * P],
                    rhs=codes[:].bitcast(FP8X4),
                    rhs_scale=plane[:],
                    start=True,
                    stop=True,
                )
            bounded = keep.tile([P, count, HALF], F32, name=f"bounded{u}_{first}")
            nc.scalar.activation(bounded[:], y[:], ACT.Tanh)
            result = keep.tile([P, count, HALF], F32, name=f"result{u}_{first}")
            nc.vector.tensor_tensor(result[:], bounded[:], vacancy[:, blocks, cols], ALU.mult)
            nc.sync.dma_start(out.rearrange("(b p) j -> p b j", p=P)[:, blocks, cols], result[:])

        for start in (0, P1 // 2):
            pick1(0, start, P1 // 2)
        for start in (0, P1 // 2):
            multiply1(0, start, P1 // 2)
        for r in range(1, PACK):
            pick1(r)
            if r >= 2:
                pick3_left(r - 2)
                pick3_right(r - 2)
            pick2(r - 1)
            if r >= 2:
                larger3(r - 2)
            multiply1(r)
            add2(r - 1)
        for t in range(2):
            for u in range(2):
                round_a3(t, u)
        pick2(3)
        pick3_late(2, 0, 0)
        pick3_late(2, 1, 0)
        add2(3)
        pick3_late(2, 0, 1)
        pick3_late(2, 1, 1)
        pick3_late(3, 0, 0)
        pick3_late(3, 1, 0)
        pick3_late(3, 0, 1)
        larger3_late(0)
        pick3_late(3, 1, 1)
        quantised = [quantise_a3(0)]
        larger3_late(1)
        quantised.append(quantise_a3(1))
        for u in range(2):
            for first in (0, 2):
                scores(u, *quantised[u], first, 2)
